import numpy as np, ml_dtypes
CORES = [10,34,74,98]
N = 4
BF = ml_dtypes.bfloat16
def gentries(a):
    return np.ascontiguousarray(a.reshape(8, 16, -1).transpose(0, 2, 1)).reshape(8, -1)
def gtable(e):
    e = np.asarray(e); return np.ascontiguousarray(e.reshape(8, -1, 16).transpose(0, 2, 1)).reshape(128, -1).astype(np.int32)
V, G, P, E, O, RO, ST = 2304, 512, 1024, 160, 32, 3, 3
W = V + (N - 1) * G; L = E + (N - 1) * O
def power(rng, *shape):
    lead = rng.integers(0, 16, shape[:-2] + (1,) + shape[-1:])
    return np.where(np.arange(16)[:, None] == lead, rng.integers(128, 256, shape), rng.integers(0, 40, shape))
def parts(rng):
    x = power(rng, N, 8, 16, V); plans = power(rng, 8, 16, P)
    share = 0.3 + 0.3 * rng.random((N, 8, 1, 1))
    nb = np.where(rng.random((N, 8, 16, V)) < share, rng.integers(V, W, (N, 8, 16, V)), rng.integers(0, V, (N, 8, 16, V)))
    pt = 2048 * rng.integers(0, 1024, (N, 8, 16, V)) + rng.integers(0, P, (N, 8, 16, V))
    req = np.ascontiguousarray(np.argsort(rng.random((N, 8, RO, V)), axis=-1)[..., :E])
    th = rng.integers(180, 281, (N, 8, 16, 1))
    return x, nb, pt, plans, req, th
def pack(x, nb, pt, plans, req, th):
    return {"x": np.ascontiguousarray(x.reshape(N, 128, V)).astype(np.float32).astype(BF), "nb": np.ascontiguousarray(nb.reshape(N, 128, V)).astype(np.int32),
            "pt": np.ascontiguousarray(pt.reshape(N, 128, V)).astype(np.int32), "plans": np.repeat(plans.reshape(1, 128, P), N, axis=0).astype(np.float32).astype(BF),
            "req": np.stack([gtable(a.reshape(8, RO * E)) for a in req]), "th": np.ascontiguousarray(th.reshape(N, 128, 1)).astype(np.int32)}
def setup_inputs(rng):
    return pack(*parts(rng))
def setup_inputs_room(rng):
    x, nb, pt, plans, req, th = parts(rng); x = np.maximum(x, 1); plans = np.maximum(plans, 1); th = th * 0
    for q in range(N):
        for g in range(8):
            o = rng.permutation(V)[:E]; req[q, g, 0] = o
            n = [int(a) for a in rng.choice(np.array([0, 1, O - 1, O, O + 1]), N - 1)]
            if q == 0: n[0] = (O, O + 1, O - 1, 0, 1, O, O + 1, E)[g]
            left = E; goals = []
            for d in range(N - 1):
                m = min(n[d], left); left -= m
                goals.append(V + d * G + rng.integers(0, G, m))
            goals.append(o[rng.integers(0, E, left)])
            nb[q, g][:, o] = rng.permutation(np.concatenate(goals))[None, :]
    return pack(x, nb, pt, plans, req, th)
def setup_inputs_ties(rng):
    x, nb, pt, plans, req, th = parts(rng)
    x = rng.integers(0, 4, x.shape); plans = rng.integers(0, 4, plans.shape); th = rng.integers(12, 19, th.shape)
    pt = 2048 * rng.integers(0, 4, pt.shape) + rng.integers(0, P, pt.shape)
    x[:, 0] = 5; x[:, 1] = 5; th[:, 0] = 80; th[:, 1] = 79; pt[:, :2] = pt[:, :2] & 2047
    x[:, 2, ::2] = 0; th[:, 2, ::2] = 0
    return pack(x, nb, pt, plans, req, th)
def setup_inputs_alike(rng):
    x, nb, pt, plans, req, th = parts(rng); s = np.arange(V)
    req[:, 0] = req[:, 0, :1]
    req[:, 3] = rng.integers(0, 40, (N, RO, E))
    req[:, 5] = rng.choice(np.array([0, V - 1, 1, V >> 1]), (N, RO, E))
    req[:, 7] = np.where(rng.random((N, RO, E)) < 0.5, req[:, 7, :, :1], req[:, 7])
    nb[:, 2] = np.where(rng.random((N, 16, V)) < 0.5, s, nb[:, 2])
    nb[:, 4] = rng.choice(np.array([0, V - 1, V, V + G - 1, W - 1]), (N, 16, V))
    nb[:, 6] = nb[:, 6, :1]
    nb[:, 1, 8:] = nb[:, 1, :8]
    return pack(x, nb, pt, plans, req, th)
def wire(rng, x, nb, plans, th, g, nxt):
    strong = np.zeros((N, V), bool)
    for q in range(N):
        t = nxt[q][nxt[q] >= 0]; strong[q, t[t < V]] = True
        e = t[t >= V] - V; strong[(q - 1 - e // G) % N, e % G] = True
    x[:, g] = np.where(strong[:, None, :], rng.integers(200, 256, (N, 16, V)), rng.integers(0, 8, (N, 16, V)))
    plans[g] = rng.integers(0, 8, (16, P)); th[:, g] = rng.integers(112, 200, (N, 16, 1))
    for q in range(N):
        seen = np.concatenate([strong[q]] + [strong[(q - d) % N, :G] for d in range(1, N)]); calm = np.nonzero(~seen)[0]
        nb[q, g] = calm[rng.integers(0, len(calm), (16, V))]
        s = np.nonzero(nxt[q] >= 0)[0]; nb[q, g][rng.integers(0, 16, len(s)), s] = nxt[q, s]
def ordered(rng, nxt, pt, req, g, a, goals, ban):
    for d in range(1, N):
        q = (a + d) % N; o = rng.permutation(V); s = o[:O]
        nxt[q, s] = V + (d - 1) * G + goals[d - 1]
        cost = np.where(np.arange(16)[:, None] == ban[d - 1][None, :], 0, rng.integers(500, 1024, (16, O)))
        pt[q, g][:, s] = 2048 * cost + (pt[q, g][:, s] & 2047)
        req[q, g, 0] = rng.permutation(o[:E]); req[q, g, 1:] = rng.choice(o[O:], (RO - 1, E))
def setup_inputs_hubs(rng):
    x, nb, pt, plans, req, th = parts(rng)
    for q in range(N):
        for g in range(8):
            own = np.concatenate([rng.permutation(G)[:3], rng.permutation(V)[:3]])
            x[q, g][:, own] = 255 - rng.integers(0, 3, (16, 6))
            goals = np.concatenate([own, V + rng.integers(0, (N - 1) * G, 2)])
            nb[q, g] = np.where(rng.random((16, V)) < 0.08, rng.choice(goals, (16, V)), nb[q, g])
    n = (N - 1) * O
    for g in (4, 5, 6):
        a = int(rng.integers(0, N)); nxt = np.full((N, V), -1, np.int64)
        goals = np.concatenate([np.zeros(1, np.int64), 1 + rng.permutation(G - 1)[:n - 1]]); ban = rng.integers(0, 16, n); ban[0] = 0
        o = rng.permutation(np.setdiff1d(np.arange(V), goals))
        ordered(rng, nxt, pt, req, g, a, goals.reshape(N - 1, O), ban.reshape(N - 1, O))
        if g == 4:
            m = 2 * E * ST; c = o[:m].reshape(2 * E, ST); nxt[a, c[:, :-1]] = c[:, 1:]
            e = np.concatenate([goals[:, None], o[m:m + n * (ST - 1)].reshape(n, ST - 1)], axis=1); nxt[a, e[:, :-1]] = e[:, 1:]
            req[a, g] = rng.choice(o[m + n * (ST - 1):], (RO, E)); req[a, g, 0] = c[:E, 0]; req[a, g, 1] = c[E:, 0]
        elif g == 5:
            hub = o[:RO]; block = o[RO:RO + (RO - 1) * E].reshape(RO - 1, E)
            nxt[a, block] = hub[:RO - 1, None]; nxt[a, goals] = hub[1]
            req[a, g, :RO - 1] = block; req[a, g, RO - 1] = rng.permutation(np.concatenate([goals, block[-1]]))[:E]
        else:
            b = o[:n]; nxt[a, goals] = b; nxt[a, b] = goals
            c = o[n:n + E]; e = o[n + E:n + 2 * E]; nxt[a, c] = e; nxt[a, e] = c
            req[a, g] = rng.choice(o[n + 2 * E:], (RO, E)); req[a, g, 0] = c
        wire(rng, x, nb, plans, th, g, nxt)
        if g == 6:
            x[a, g][ban, b] = rng.integers(0, 8, n)
            cost = np.where(np.arange(16)[:, None] == ban[None, :], 1023, rng.integers(0, 301, (16, n)))
            pt[a, g][:, b] = 2048 * cost + (pt[a, g][:, b] & 2047)
    return pack(x, nb, pt, plans, req, th)
def setup_inputs_spread(rng):
    x, nb, pt, plans, req, th = parts(rng)
    x = np.minimum((np.exp2(8 * rng.random((N, 8, 1, V))) * rng.random((N, 8, 16, V))).astype(np.int64), 255)
    plans = np.minimum((np.exp2(8 * rng.random((8, 1, P))) * rng.random((8, 16, P))).astype(np.int64), 255)
    x[..., 0] = 255; x[..., V - 1] = 255
    cost = np.minimum(np.exp2(10 * rng.random(pt.shape)).astype(np.int64) - 1, 1023)
    pt = 2048 * cost + rng.integers(0, P, pt.shape); pt[..., 0] = 2048 * 1023 + P - 1
    th = (np.exp2(5 + 5 * rng.random((N, 8, 1, 1))) * (0.5 + rng.random((N, 8, 16, 1)))).astype(np.int64)
    th[:, 0] = rng.integers(0, 4081, (N, 16, 1))
    for g, n, lo, t0, t1, u0, u1, k0, k1 in ((5, 8, 200, 3900, 4080, 0, 12, 500, 200), (6, 15, 240, 3000, 3700, 22, 26, 900, 300), (7, 16, 240, 3930, 3990, 0, 0, 500, 0)):
        heavy = rng.permutation(16)[:, None] < n
        x[:, g] = np.where(heavy, rng.integers(lo, 256, (N, 16, V)), rng.integers(0, 4, (N, 16, V)))
        plans[g] = np.where(heavy, rng.integers(lo, 256, (16, P)), rng.integers(0, 4, (16, P)))
        th[:, g] = np.where(heavy, rng.integers(t0, t1 + 1, (N, 16, 1)), rng.integers(u0, u1 + 1, (N, 16, 1)))
        cost = np.where(heavy, rng.integers(k0, 1024, (N, 16, V)), rng.integers(0, k1 + 1, (N, 16, V)))
        pt[:, g] = 2048 * cost + (pt[:, g] & 2047)
    return pack(x, nb, pt, plans, req, th)
def check_inputs(d):
    bad = []
    for k in ("x", "plans"):
        v = np.asarray(d[k]).astype(np.float32)
        if not (np.min(v) >= 0 and np.max(v) <= 255 and np.all(v == np.floor(v))): bad.append("range of " + k)
    for k, hi in (("nb", W - 1), ("pt", 2048 * 1023 + 2047), ("req", V - 1), ("th", 4080)):
        if not (np.min(d[k]) >= 0 and np.max(d[k]) <= hi): bad.append("range of " + k)
    if np.max(np.asarray(d["pt"]).astype(np.int64) & 2047) >= P: bad.append("plan numbers in pt")
    v = np.asarray(d["plans"]).astype(np.float32)
    if not np.all(v == v[:1]): bad.append("plans alike on all ranks")
    return bad
def chains(w, nbg, ptg, tg, frozen, first, ban):
    lanes = np.arange(L); ch = np.arange(16)[:, None]; mark = np.array(frozen)
    got = np.zeros((ST, L), bool); where = np.zeros((ST, L), np.int64); plan = np.zeros((ST, L), np.int64)
    good = np.zeros(L, bool); order = np.full(L, -1, np.int64); live = first >= 0; s = first
    for k in range(ST):
        at = np.where(live, s, 0)
        idx = np.nonzero(live & ~mark[at])[0]
        u, j = np.unique(at[idx], return_index=True)
        reach = np.zeros(L, bool); reach[idx[j]] = True; mark[u] = True
        q = nbg[:, at]
        p = w[:, q]
        total = np.add.reduce(p, axis=1); over = total > tg
        price = total + (ptg[:, at] >> 11) + 4096 * over + 16384 * (ch == ban[None, :])
        c = np.argmin(price, axis=0)
        got[k] = reach; where[k] = at; plan[k] = ptg[c, at] & 2047
        stuck = over[c, lanes]
        b = q[np.argmax(p[c, :, lanes], axis=1), lanes]
        good = good | (reach & ~stuck)
        order = np.where(reach & stuck & (b >= V), (b - V) * 16 + c, order)
        live = reach & stuck & (b < V); s = b; ban = c
    return got, where, plan, good, order
def reference(x, nb, pt, plans, req, th):
    now = x.astype(np.float32).astype(np.int64).reshape(N, 8, 16, V); nbl = nb.astype(np.int64).reshape(N, 8, 16, V); ptl = pt.astype(np.int64).reshape(N, 8, 16, V)
    pl = plans.astype(np.float32).astype(np.int64).reshape(N, 8, 16, P); t = th.astype(np.int64).reshape(N, 8, 16, 1)
    rq = np.stack([gentries(a) for a in req]).astype(np.int64).reshape(N, 8, RO, E)
    frozen = np.zeros((N, 8, V), bool); inbox = np.full((N, 8, N - 1, O), -1, np.int64)
    for rnd in range(RO):
        new = np.array(now); nextbox = np.full((N, 8, N - 1, O), -1, np.int64)
        for r in range(N):
            w = np.concatenate([now[r]] + [now[(r - d) % N][:, :, :G] for d in range(1, N)], axis=2)
            for g in range(8):
                box = inbox[r, g].reshape(-1)
                first = np.concatenate([rq[r, g, rnd], np.where(box >= 0, box >> 4, -1)])
                ban = np.concatenate([np.full(E, -1, np.int64), np.where(box >= 0, box & 15, -1)])
                got, where, plan, good, order = chains(w[g], nbl[r, g], ptl[r, g], t[r, g], frozen[r, g], first, ban)
                for d in range(1, N):
                    i = np.nonzero((order >= (d - 1) * 16 * G) & (order < d * 16 * G))[0][:O]
                    good[i] = True; nextbox[(r - d) % N, g, d - 1, :len(i)] = order[i] - (d - 1) * 16 * G
                for k in range(ST):
                    m = got[k] & good
                    new[r, g][:, where[k][m]] = pl[r, g][:, plan[k][m]]
                frozen[r, g][where[0][got[0] & ~good]] = True
        now = new; inbox = nextbox
    return {"y": now.reshape(N, 128, V).astype(np.float32).astype(BF)}

import numpy as np
from concourse.bass import DstId, RemoteDMATransfer
from concourse.mybir import dt, AluOpType, AxisListType, ActivationFunctionType
A = AluOpType
FN = ActivationFunctionType

N, V, GH, PL, RO, ST = 4, 2304, 512, 1024, 3, 3
DW = 768
DM = 256
U = 2.0 ** -20
NCS = (10, 16, 16)
CHUNKS = (((0, 6), (6, 4)), ((0, 8), (8, 8)), ((0, 8), (8, 8)))
PIECE = 32
ONV = {(1, 0, 0): (1, 3), (2, 0, 0): (1, 3)}
BS, BD, BM = 8192.0, 512.0, 131072.0
OWN = 1.0 / (V - 0.5)

F32, BF, F16, I32, U16 = "float32", "bfloat16", "float16", "int32", "uint16"
SCRATCH = {}


def _s(names, cols, d, where="sbuf"):
    for nm in names.split():
        SCRATCH[nm] = (where, [128] + (list(cols) if isinstance(cols, list) else [cols]), d)


_s("w0 w1 w2", DW + V + 3 * GH, BF)
_s("mk0 mk1 mk2", DM + V, F32)
_s("nbs pts", V, I32)
_s("pls", 2 * PL, BF)
_s("rq", 32, I32)
_s("ths", 8, I32)
_s("ci", 288, F32)
_s("k16", 256, F32)
_s("k15 jg g8 idf blkf tmp tmq", 128, F32)
_s("pa", 16, F32)
_s("pii", 16, I32)
_s("col", 32, F32)
_s("idn lsel", 1024, BF)
_s("dban c2a blk2 blkw blkm blk1 trim d0min d0add selg", 128, BF)
_s("ca tha k2047", 128, F16)
_s("d0max", 16 * PIECE, BF)
_s("selb diag", 256, BF)
_s("selm d0r", 96, BF)
_s("poss", 144, F32)
_s("bc16 bcu", 16, U16)
_s("pza pzf", 256, F32)
for _h in "01":
    _s("q" + _h, 128, U16)
    _s(" ".join(x + _h for x in ("qf", "co", "fl", "zb", "zy", "sb")), 128, F16)
    _s("sy" + _h, 256, F16)
    _s("p" + _h, 2048, BF)
    _s("m" + _h, 2048, F16)
    _s(" ".join(x + _h for x in ("ptf", "thr", "key", "fw", "sly")), 128, F32)
    _s("slb" + _h, 64, F32)
    _s(" ".join(x + _h for x in ("ov", "oh", "ohi")), 128, BF)
    _s("f" + _h, 24, I32)
_s("at plu offw", 144, U16)
_s("offm", 208, U16)
_s("atf live reach bb bs cc stk cont", 144, F32)
_s("sm", 40 * 48, F32)
_s("smi", 64, I32)
_s("fv", 32, F32)
_s("fd fs", 48, BF)
_s("atr", 256, F16)
_s("em", 256, BF)
_s("e3", [16, 256], BF)
_s("dsel vx va", 256, F32)
_s("pw", 768, BF)
_s("ms0 ms1", DM + 96, F32)
_s("in0 in1 isel", 96, F32)
_s("stp", 128, BF)
_s("P0 P1 Q0 Q1 B0 B1 DD XX", 512, F32, "psum")
PART = {"d0r0": ("d0r", 0, 48), "d0r1": ("d0r", 48, 48), "pos": ("poss", 0, 48), "posw": ("poss", 48, 48), "posk": ("poss", 96, 48)}
for _h in "01":
    for _j, _n in enumerate(("fi", "fa", "fc")):
        PART[_n + _h] = ("f" + _h, 8 * _j, 8)
PSUM = ("P0", "P1", "Q0", "Q1", "B0", "B1", "DD", "XX")
DMAS = ["l%d" % i for i in range(11)]
SEMAPHORES = ["cv", "ca", "ct", "cg"] + DMAS + ["gh0", "gh1", "gh2", "od0", "od1", "s0", "s1", "s2", "s3", "s4"]

CY, PE, GA, SC = 1.0e-3, 0.6e-3, 1.35e-3, 3.3e-3
LSAME, LCROSS = 0.08, 0.15
TRIES = 300
ORDER = []


def build(T, rank, topo):
    ops = []
    size = {F32: 4, I32: 4, BF: 2, F16: 2, U16: 2}

    def v(name, lo=0, hi=None, step=1, n=128):
        name, at, cols = PART.get(name) or (name, 0, SCRATCH[name][1][1])
        lo, hi = at + lo, at + (cols if hi is None else hi)
        ap = T[name][0:n, lo:hi] if step == 1 else T[name][0:n, lo:hi:step]
        return (ap, [(name, lo, hi)], len(range(lo, hi, step)), size[SCRATCH[name][2]], name in PSUM, False)

    def e3(a0, a1, lo, hi):
        ap = T.e3[:, a0, lo:hi] if a1 == a0 + 1 else T.e3[:, a0:a1, lo:hi]
        return (ap, [("e3", a * 256 + lo, a * 256 + hi) for a in range(a0, a1)], (a1 - a0) * (hi - lo), 2, False, False)

    def ind(win, off):
        return (win[0].indirect(off[0]), win[1] + off[1], 16 * off[2], win[3], False, True)

    def add(e, c, r, w, fn, tok=None, lat=0.0):
        ops.append({"e": e, "c": c, "r": r, "w": w, "fn": fn, "tok": tok, "lat": lat})

    def regs(*xs):
        return [q for x in xs if isinstance(x, tuple) for q in x[1]]

    def ap(x):
        return x[0] if isinstance(x, tuple) else x

    def cost(out, ins, two=False):
        n = max(x[2] for x in ins)
        if out[5]:
            return 0.06 + SC * n
        if any(x[5] for x in ins):
            return 0.06 + GA * n
        if two:
            return CY * max(64, n * (1 if any(x[4] for x in ins) else 2))
        return CY * max(64, n * (0.5 if out[3] == 2 and all(x[3] == 2 for x in ins) else 1))

    def ts(out, x, s1, s2, o0, o1=None):
        if o1 is None:
            add("v", cost(out, [x]), regs(x, s1), out[1], lambda Q: Q.tensor_scalar(out[0], x[0], ap(s1), None, o0))
        else:
            add("v", cost(out, [x]), regs(x, s1, s2), out[1], lambda Q: Q.tensor_scalar(out[0], x[0], ap(s1), ap(s2), o0, o1))

    def tt(out, x, y, o):
        add("v", cost(out, [x, y], True), regs(x, y), out[1], lambda Q: Q.tensor_tensor(out[0], x[0], y[0], o))

    def cp(out, x):
        r, w = (out[1][1:], out[1][:1]) if out[5] else ([], out[1])
        add("v", cost(out, [x]), r + regs(x), w, lambda Q: Q.tensor_copy(out[0], x[0]))

    def scan(out, d0, d1, o0, o1):
        add("v", cost(out, [d0, d1]), regs(d0, d1), out[1], lambda Q: Q.tensor_tensor_scan(out[0], d0[0], d1[0], 0.0, o0, o1))

    def ms(out, c):
        add("v", CY * max(64, out[2] * out[3] / 4), [], out[1], lambda Q: Q.memset(out[0], c))

    def act(out, x, bias=0.0, scale=1.0):
        c = 0.07 + GA * x[2] if x[5] else CY * max(64, x[2]) + 0.05
        add("a", c, regs(x, bias), out[1], lambda Q: Q.activation(out[0], x[0], FN.Identity, bias=ap(bias), scale=scale))

    def put(out, x):
        add("a", 0.07 + SC * x[2], out[1][1:] + x[1], out[1][:1], lambda Q: Q.activation(out[0], x[0], FN.Silu))

    def mm(lst):
        def fn(Q):
            for o, l, r, s, t in lst:
                i = Q.matmul(o[0], l[0], r[0], s, t)
            return i
        c = sum(PE * max(min(64, l[2]), r[2]) * (4 if l[3] == 4 else 1) for o, l, r, s, t in lst)
        add("t", c + 0.03, [q for o, l, r, s, t in lst for q in l[1] + r[1]], [q for o, l, r, s, t in lst for q in o[1]], fn)

    def iota(out, pat, base, chm):
        add("g", 0.13 + 2 * CY * out[2], [], out[1], lambda Q: Q.iota(out[0], pat, base, chm, allow_small_or_imprecise_dtypes=True))

    nd = [0]

    def dma(e, out, in_, r, w, us):
        sem = DMAS[nd[0]]
        nd[0] += 1
        add(e, 0.06, r, w, lambda Q: Q.dma_start(out, in_), (sem, 16), us)

    me = T.cores[rank]
    others = [T.cores[(rank + d) % N] for d in range(1, N)]
    eng = [e for e in topo.engines(me, others[0]) if all(e in topo.engines(me, o) for o in others)]

    def dst(c):
        a = topo.addr(c)
        return DstId(rid=a[0], pnc=a[1])

    def bits(es):
        return sum(1 << e for e in es)

    def send_ghosts(r):
        name = "w%d" % r
        tr = RemoteDMATransfer(dst_ids=[dst(o) for o in others], dma_engine_mask=bits(eng), remote_sem=T.sem["gh%d" % r],
                               srcs=[T[name][:, DW:DW + GH]],
                               dsts=[T[name][:, DW + V + d * GH:DW + V + (d + 1) * GH] for d in range(N - 1)])
        add("g", 1.0, [(name, DW, DW + GH)], [("sent%d" % r, 0, 1)], lambda Q: Q.remote_dma_fused([tr], local_sem=T.sem["s%d" % r]),
            ("s%d" % r, len(eng)), 3.0)
        add("x", 0.0, [("sent%d" % r, 0, 1)], [(name, DW + V, DW + V + 3 * GH)], None, ("gh%d" % r, (N - 1) * len(eng)), 1.0)

    def send_orders(r):
        hf = len(eng) // 2
        parts = [eng[:hf], eng[hf:hf + hf // 2], eng[hf + hf // 2:]]
        trs = [RemoteDMATransfer(dst_ids=[dst(T.cores[(rank - d - 1) % N])], dma_engine_mask=bits(parts[d]), remote_sem=T.sem["od%d" % r],
                                 srcs=[T["ms%d" % r][:, DM + 32 * d:DM + 32 * d + 32]], dsts=[T["in%d" % r][:, 32 * d:32 * d + 32]])
               for d in range(N - 1)]
        add("g", 1.0, [("ms%d" % r, DM, DM + 96)], [("sento%d" % r, 0, 1)], lambda Q: Q.remote_dma_fused(trs, local_sem=T.sem["s%d" % (3 + r)]),
            ("s%d" % (3 + r), len(eng)), 2.0)
        add("x", 0.0, [("sento%d" % r, 0, 1)], [("in%d" % r, 0, 96)], None, ("od%d" % r, len(eng)), 1.0)

    dma("s", T.w0[:, DW:DW + GH], T.x[:, 0:GH], [], [("w0", DW, DW + GH)], 2.2)
    dma("s", T.rq[:, 0:30], T.req[:], [], [("rq", 0, 32)], 2.2)
    dma("s", T.nbs[:], T.nb[:], [], [("nbs", 0, V)], 7.0)
    dma("s", T.w0[:, DW + GH:DW + V], T.x[:, GH:V], [], [("w0", DW + GH, DW + V)], 9.0)
    dma("s", T.pts[:], T.pt[:], [], [("pts", 0, V)], 13.0)
    dma("a", T.ths[:, 0:1], T.th[:], [], [("ths", 0, 8)], 2.5)
    dma("s", T.pls[:, 0:PL], T.plans[:], [], [("pls", 0, PL)], 14.0)
    dma("s", T.pls[:, PL:2 * PL], T.plans[:], [], [("pls", PL, 2 * PL)], 15.0)
    send_ghosts(0)

    iota(v("ci"), [[1, 288]], 0, 0)
    add("g", 0.14, [], [("pii", 0, 1)], lambda Q: Q.iota(T.pii[:, 0:1], [[0, 1]], 0, 1))
    iota(v("k16"), [[0, 16], [1, 16]], 0, 0)
    iota(v("pa", 0, 8), [[-16, 8]], 0, 1)
    iota(v("jg"), [[1, 8], [0, 16]], 0, 0)
    iota(v("g8"), [[0, 16], [1, 8]], 0, 0)
    cn = {}

    def c(name):
        if name not in cn:
            cn[name] = len(cn)
        return v("col", cn[name], cn[name] + 1)
    cp(c("p"), v("pii", 0, 1))
    ts(v("pii", 4, 5), v("pii", 0, 1), 15, None, A.bitwise_and)
    ts(v("pii", 8, 9), v("pii", 0, 1), 4, None, A.arith_shift_right)
    cp(c("b"), v("pii", 4, 5))
    cp(c("g"), v("pii", 8, 9))
    for r in range(RO):
        for j in range(8):
            act(v("mk%d" % r, DM + 288 * j, DM + 288 * (j + 1)), v("ci"), bias=288.0 * j - 1152.0)
    ci = v("ci", 0, 128)
    ts(v("pos"), v("ci", 0, 48), 16.0, c("b"), A.mult, A.add)
    ts(v("posw"), v("pos"), -(1152.0 + DW), None, A.add)
    ts(v("posk"), v("pos"), -(1152.0 + DM), None, A.add)
    cp(v("bc16"), v("ci", 0, 16))
    ts(v("bcu"), v("ci", 0, 16), 16.0, 15.0, A.mult, A.add)
    ms(v("pza"), 2040.0)
    ms(v("pzf"), 2044.0)
    ms(v("tmp", 0, 16), 0.5)
    ms(v("tmp", 16, 32), 0.0)
    ms(v("tmp", 16, 17), 1.0)
    scan(v("tmp", 32, 48), v("tmp", 0, 16), v("tmp", 16, 32), A.mult, A.add)
    ts(v("diag"), v("k16"), c("b"), None, A.is_equal)
    tt(v("tmp", 48, 64), v("tmp", 32, 48), v("diag", 0, 16), A.mult)
    add("v", 0.07, [("tmp", 48, 64)], c("w")[1], lambda Q: Q.tensor_reduce(c("w")[0], v("tmp", 48, 64)[0], AxisListType.X, A.add))
    ts(c("thr"), c("w"), 2.5, None, A.mult)
    ts(c("bd"), c("b"), 15.0, BD, A.is_lt, A.mult)
    ts(c("bm"), c("b"), 15.0, BM, A.is_lt, A.mult)
    ts(c("b1"), c("b"), 1.0, None, A.add)
    ts(v("blkw"), v("jg"), c("g"), c("w"), A.is_equal, A.mult)
    ts(v("blk2"), v("jg"), c("g"), 2.0, A.is_equal, A.mult)
    ts(v("blkm"), v("jg"), c("g"), 0.25, A.is_equal, A.mult)
    ts(v("selb"), v("k16"), c("b"), -4 * BD, A.is_equal, A.mult)
    ts(v("vx"), v("k16"), c("b1"), BD, A.is_equal, A.mult)
    tt(v("selb"), v("selb"), v("vx"), A.add)
    ts(v("selm"), v("selb", 0, 96), BM / BD, None, A.mult)
    scales = {"v": 16 * U, "c": 256 * U, "u": U, "mu": -U, "4": 4.0, "k": 1024.0, "mk": -2048.0, "1": 1.0}
    idn = {}
    for j, nm in enumerate(scales):
        idn[nm] = j * 128
        ts(v("idn", j * 128, j * 128 + 128), ci, c("p"), scales[nm], A.is_equal, A.mult)

    def I(nm, n=128):
        return v("idn", idn[nm], idn[nm] + n, 1, n)
    ts(v("idf"), ci, c("p"), None, A.is_equal)
    ts(c("ca"), c("b"), 16.0, 24576.0, A.mult, A.add)
    ts(c("c2"), c("b"), 16.0, 128.0, A.mult, A.add)
    ts(c("th"), v("ths", 0, 1), -2048.0, None, A.add)
    ts(v("ca"), ci, 0.0, c("ca"), A.mult, A.add)
    ts(v("c2a"), ci, 0.0, c("c2"), A.mult, A.add)
    ts(v("tha"), ci, 0.0, c("th"), A.mult, A.add)
    ms(v("k2047"), 2047.0)
    for a in range(8):
        ts(v("lsel", a * 128, a * 128 + 128), v("k16", 0, 128), v("pa", a, a + 1), None, A.is_equal)
    ts(v("k15"), v("k16", 0, 128), -1.0, 15.0, A.mult, A.add)
    ms(v("d0max"), 1.0)
    ms(v("d0max", 0, None, 16), -8192.0)
    ms(v("d0min"), 0.0)
    ms(v("d0min", 0, None, 16), 64.0)
    ms(v("d0add"), 1.0)
    ms(v("d0add", 0, None, 16), 0.0)
    ts(c("g1"), c("g"), 1.0, None, A.add)
    ts(v("tmp"), v("g8"), c("g"), -4 * BS, A.is_equal, A.mult)
    ts(v("tmq"), v("g8"), c("g1"), BS, A.is_equal, A.mult)
    tt(v("selg"), v("tmp"), v("tmq"), A.add)
    ts(c("cc"), c("g"), 7.0, -BS, A.is_lt, A.mult)
    ts(c("cb"), c("cc"), 2048.0, None, A.add)
    ts(c("cf"), c("cc"), 2048.0 - 1152.0, None, A.add)
    ts(c("cv"), c("cc"), 2048.0 + 256.0, None, A.add)
    ts(c("co"), c("cb"), OWN, None, A.mult)
    ts(c("cy"), c("cc"), 1024.0, None, A.add)
    ts(c("c4"), c("cc"), 4096.0, None, A.mult)
    for h in "01":
        ms(v("key" + h), 0.0)
        ms(v("fw" + h), 0.0)
        ms(v("fa" + h), 0)
    ts(v("blk1"), v("jg"), c("g"), None, A.is_equal)
    ts(v("blkf"), v("jg"), c("g"), None, A.is_equal)
    ts(v("tmp"), v("k16", 0, 128), c("b"), -1.0, A.is_le, A.mult)
    tt(v("trim"), v("tmp"), v("blkf"), A.mult)
    ts(c("p1"), c("p"), -1.0, None, A.add)
    ts(c("nf"), c("b"), 0.0, -4.0, A.is_gt, A.mult)
    ts(v("tmq"), ci, c("p1"), c("nf"), A.is_equal, A.mult)
    tt(v("dban"), v("tmq"), I("4"), A.add)
    ts(c("cs"), c("b"), 4096.0, None, A.mult)
    ms(v("stp", 0, 32), 0.0)
    for j in range(2):
        ms(v("d0r%d" % j), 1.0)
        ms(v("d0r%d" % j, 0, None, NCS[j]), 0.0)
        ms(v("ms%d" % j, DM), 0.0)

    slot = [0]

    def sm(n=16):
        slot[0] = (slot[0] + 1) % 40
        return v("sm", slot[0] * 48, slot[0] * 48 + n)
    om = [0]
    frozen = []

    def offsets(x, lo, hi):
        y, off = sm(hi - lo), v("offm", om[0], om[0] + hi - lo)
        om[0] += 16
        tt(y, x, v("pos", lo, hi), A.add)
        cp(off, y)
        return off

    def mark(r, o, lo, hi, flag, value):
        t, x = sm(hi - lo), sm(hi - lo)
        tt(t, v("atf", o + lo, o + hi), v("posk", lo, hi), A.subtract)
        tt(x, t, flag, A.mult)
        off = offsets(x, lo, hi)
        put(ind(v("mk%d" % r), off), v(value, 0, 16 * (hi - lo)))
        return off

    def first(r, o, nc, a0, marks, live, outs):
        W = 16 * nc
        cp(v("atr", 0, W), ind(v("mk%d" % r, DM), v("at", o, o + nc)))
        lst = []
        for lo, hi, bound in marks:
            ts(v("em", lo, hi), v("atr", lo, hi), bound, None, A.is_ge)
        if marks:
            lst.append((v("DD", 0, W), v("blkm"), v("em", 0, W)))
        for a in range(a0, nc):
            if live:
                ts(e3(a, a + 1, 0, W - 16 * a), v("atr", 16 * a, W), v("atf", o + a, o + a + 1), v("live", o + a, o + a + 1), A.is_equal, A.mult)
            else:
                ts(e3(a, a + 1, 0, W - 16 * a), v("atr", 16 * a, W), v("atf", o + a, o + a + 1), None, A.is_equal)
        tail = (v("DD", 16 * a0, W), v("blkw"), e3(a0, nc, 0, 16))
        if not marks:
            lst.append(tail)
        for a in range(a0, nc - 1):
            lst.append((v("DD", 16 * (a + 1), W), v("blk2"), e3(a, a + 1, 16, W - 16 * a)))
        if marks:
            lst.append(tail)
        lst = [x + (j == 0, j == len(lst) - 1) for j, x in enumerate(lst)]
        for j in range(0, len(lst), 3):
            mm(lst[j:j + 3])
        scan(v("dsel", 0, W), v("selb", 0, W), v("DD", 0, W), A.add, A.max)
        for out in outs:
            ts(out, v("dsel", 15, W, 16), c("bd"), c("thr"), A.subtract, A.is_lt)

    def requests(r):
        o = 48 * r
        first(r, o, 10, 0, [], False, [v("live", o, o + 10)] + ([v("reach", 0, 10)] if r == 0 else []))
        mark(r, o, 0, 10, v("live", o, o + 10), "pza")

    for r in range(RO):
        cp(v("at", 48 * r, 48 * r + 10), v("rq", 10 * r, 10 * r + 10))
        ts(v("atf", 48 * r, 48 * r + 10), v("rq", 10 * r, 10 * r + 10), -1152.0, None, A.add)
    requests(0)

    def chunk(r, k, h):
        a0, na = CHUNKS[r][h]
        n = 16 * na
        nc = NCS[r]
        o = 48 * r + k * nc + a0
        H = str(h)
        last = r == RO - 1

        def A_(nm):
            return v(nm + H, 0, n)

        def C_(nm, lo=0, hi=128, step=1):
            return v(nm + H, lo, hi, step, n)
        at = v("at", o, o + na)
        cp(A_("q"), ind(v("nbs"), at))
        cp(A_("ptf"), ind(v("pts"), at))
        ts(A_("qf"), A_("q"), -2048.0, None, A.add)
        ts(A_("co"), A_("ptf"), 1.0 / 2048, 1024.0, A.mult, A.add)
        P, thp, qT, Y = C_("P"), C_("P", 128, 256), C_("Q", 128, 256), C_("Q", 256, 384)
        mm([(thp, A_("co"), I("c"), True, False), (thp, v("tha", 0, n), I("c"), False, False), (thp, v("c2a", 0, n), I("u"), False, True)])
        act(C_("thr"), thp)
        mm([(qT, A_("qf"), I("1"), True, True)])
        mm([(Y, A_("ptf"), v("idf"), True, False), (Y, A_("co"), I("mk"), False, False), (Y, v("k2047", 0, n), I("k"), False, False)])
        lst = [(P, v("ca", 0, n), I("u"), True, False), (P, A_("co"), I("c"), False, False)]
        if k > 0:
            lst.append((P, I("4", n), C_("oh"), False, False))
        elif r > 0 and h == 1:
            lst.append((P, v("stp"), v("dban"), False, False))
        mm(lst)
        win = v("w%d" % r, DW)
        for lo in range(0, n, PIECE):
            hi = min(n, lo + PIECE)
            if lo // PIECE in ONV.get((r, k, h), ()):
                ts(v("p" + H, 16 * lo, 16 * hi), ind(win, v("q" + H, lo, hi)), 16.0, -2048.0, A.mult, A.add)
            else:
                act(v("p" + H, 16 * lo, 16 * hi), ind(win, v("q" + H, lo, hi)), bias=-2048.0, scale=16.0)
            scan(v("m" + H, 16 * lo, 16 * hi), v("d0max", 0, 16 * (hi - lo)), v("p" + H, 16 * lo, 16 * hi), A.add, A.max)
        for j in range(0, 16, 4):
            mm([(P, v("p" + H, i, 16 * n, 16), I("v"), False, False) for i in range(j, j + 4)])
        ts(A_("fl"), v("m" + H, 15, 16 * n, 16), 24568.5, None, A.add)
        mm([(P, v("m" + H, 15, 16 * n, 16), I("u"), False, False), (P, A_("fl"), I("mu"), False, True)])
        tt(C_("ov"), P, C_("thr"), A.is_gt)
        tt(C_("key"), P, C_("ov"), A.add)
        mm([(Y, I("k", n), C_("ov"), False, True)])
        scan(C_("fw"), v("d0min", 0, 128, 1, n), C_("key"), A.add, A.min)
        ts(C_("fi", 0, 8), C_("fw", 15, 128, 16), 1.0 / U, None, A.mult)
        ts(C_("fa", 0, 8), C_("fi", 0, 8), 15, None, A.bitwise_and)
        tt(v("ohi" + H), ind(v("fa" + H), v("bc16", 0, 8)), v("k15"), A.is_equal)
        tt(C_("zb"), qT, C_("ohi"), A.mult)
        scan(C_("sb"), v("d0add", 0, 128, 1, n), C_("zb"), A.mult, A.add)
        mm([(v("B" + H, 8 * a, 8 * a + 8), v("lsel", 128 * a, 128 * a + 128, 1, n), C_("sb", 15, 128, 16), True, True) for a in range(na)])
        scan(v("slb" + H, 0, 8 * na), v("selg", 0, 8 * na), v("B" + H, 0, 8 * na), A.add, A.max)
        b = v("slb" + H, 7, 8 * na, 8)
        if k < ST - 1:
            ts(v("at", o + nc, o + nc + na), b, c("cb"), float(V - 1), A.add, A.min)
            act(v("atf", o + nc, o + nc + na), b, c("cf"))
        act(v("bs", o, o + na), b, c("co"), OWN)
        if not last:
            act(v("bb", o, o + na), b, c("cv"))
        tt(v("oh" + H), ind(v("fw" + H), v("bcu", 0, 8)), v("key" + H), A.is_equal)
        tt(C_("zy"), Y, C_("oh"), A.mult)
        scan(C_("sy"), v("d0add", 0, 128, 1, n), C_("zy"), A.mult, A.add)
        pay = 1 if last else 2
        if not last:
            ts(C_("fc", 0, 8), C_("fi", 0, 8), 4, 15, A.arith_shift_right, A.bitwise_and)
            ts(C_("sy", 143, 256, 16), C_("fc", 0, 8), 0.0, None, A.add)
        wd = 8 * pay
        mm([(v("B" + H, 128 + wd * a, 128 + wd * (a + 1)), v("lsel", 128 * a, 128 * a + 128, 1, n), C_("sy", 15, 128 * pay, 16), True, True)
            for a in range(na)])
        scan(v("sly" + H, 0, wd * na), v("selg", 0, wd * na), v("B" + H, 128, 128 + wd * na), A.add, A.max)
        ts(v("plu", o, o + na), v("sly" + H, 7, wd * na, wd), c("cy"), None, A.add)
        if not last:
            act(v("cc", o, o + na), v("sly" + H, 15, wd * na, wd), c("c4"), 4096.0)

    for r in range(RO):
        nc = NCS[r]
        o0 = 48 * r
        last = r == RO - 1
        n3 = 3 * nc

        def B(nm, k, k1=None):
            return v(nm, o0 + k * nc, o0 + (k + 1 if k1 is None else k1) * nc)

        def part(x, k):
            lo = x[1][0][1]
            return v(x[1][0][0], lo + k * nc, lo + (k + 1) * nc)
        if r > 0:
            inb = v("in%d" % (r - 1))
            ts(v("stp", 32, 128), inb, c("cs"), None, A.is_ge)
            scan(v("isel"), v("selm"), inb, A.add, A.max)
            ts(v("smi", 0, 6), v("isel", 15, 96, 16), c("bm"), None, A.subtract)
            ts(v("smi", 16, 22), v("smi", 0, 6), GH - 1, None, A.bitwise_and)
            ts(v("at", o0 + 10, o0 + 16), v("smi", 16, 22), 0.0, None, A.add)
            ts(v("atf", o0 + 10, o0 + 16), v("smi", 16, 22), -1152.0, None, A.add)
            ts(v("live", o0 + 10, o0 + 16), v("smi", 0, 6), 0.0, None, A.is_gt)
        for k in range(ST):
            chunk(r, k, 0)
            chunk(r, k, 1)
            if r == 0 and k == 0:
                dma("s", T.w1[:, DW:DW + V], T.x[:], [("p0", 0, 1)], [("w1", DW, DW + V)], 5.0)
            if r == 1 and k == 0:
                dma("s", T.w2[:, DW:DW + V], T.w1[:, DW:DW + V], [("p0", 0, 1), ("w1", DW, DW + V)], [("w2", DW, DW + V)], 5.0)
            if k > 0 or r > 0:
                t = sm(nc)
                if k == 0:
                    first(r, o0, nc, 10, [(0, 160, 2042.0), (160, 256, 2000.0)], True, [t])
                else:
                    first(r, o0 + k * nc, nc, 0, [(0, 16 * nc, 2000.0)], True, [t])
                tt(B("reach", k), t, B("live", k), A.mult)
                if k == 0:
                    mark(r, o0, 10, 16, v("reach", o0 + 10, o0 + 16), "pza")
                elif k == 1:
                    mark(r, o0 + nc, 0, nc, B("reach", 1), "pza")
            ts(B("stk", k), B("plu", k), 1024.0, None, A.is_ge)
            tt(B("cont", k), B("bs", k), B("stk", k), A.is_lt)
            if k < ST - 1:
                tt(B("live", k + 1), B("reach", k), B("cont", k), A.mult)
            act(v("pw", 16 * k * nc, 16 * (k + 1) * nc), ind(v("pls"), B("plu", k)))
        z, ask, ab, early, rb, e2, e = sm(2 * nc), sm(2 * nc), sm(2 * nc), sm(nc), sm(nc), sm(nc), sm(nc)
        tt(z, B("reach", 0, 2), B("stk", 0, 2), A.mult)
        tt(ask, z, B("live", 1, 3), A.subtract)
        tt(ab, ask, B("bs", 0, 2), A.mult)
        tt(early, part(ab, 0), part(ab, 1), A.add)
        tt(rb, B("reach", 2), B("bs", 2), A.mult)
        tt(e2, rb, B("stk", 2), A.mult)
        tt(e, e2, early, A.add)
        dd = v("smi", 32 + 16 * (r % 2), 32 + 16 * (r % 2) + nc)
        ts(dd, e, 1.0 / (OWN * GH), 0.001, A.mult, A.add)
        for d in range(3):
            ts(v("fd", d * nc, (d + 1) * nc), dd, 5.0 + d, None, A.is_equal)
        scan(v("fs", 0, n3), v("d0r%d" % min(r, 1), 0, n3), v("fd", 0, n3), A.mult, A.add)
        mm([(v("XX", 0, n3), v("blk1"), v("fs", 0, n3), True, False), (v("XX", 0, n3), v("trim"), v("fd", 0, n3), False, True)])
        rm, r1, ro, good = sm(n3), sm(nc), sm(nc), sm(nc)
        tt(rm, v("XX", 0, n3), v("fd", 0, n3), A.mult)
        tt(r1, part(rm, 0), part(rm, 1), A.add)
        tt(ro, r1, part(rm, 2), A.add)
        s1, s3, end2, g2, succ, s32 = sm(2 * nc), sm(nc), sm(nc), sm(nc), sm(nc), sm(nc)
        tt(s1, B("reach", 0, 2), B("live", 1, 3), A.subtract)
        tt(s3, part(s1, 0), part(s1, 1), A.add)
        tt(g2, B("reach", 2), B("cont", 2), A.is_gt)
        tt(succ, g2, s3, A.add)
        act(s32, succ, 0.0, 32.0)
        tt(good, ro, s32, A.is_lt)
        ta, ra, xs, ys = sm(n3), sm(n3), sm(n3), sm(n3)
        tt(ta, B("atf", 0, 3), v("posw", 0, n3), A.subtract)
        tt(ra, ta, B("reach", 0, 3), A.mult)
        for k in range(ST):
            tt(part(xs, k), part(ra, k), good, A.mult)
        tt(ys, xs, v("pos", 0, n3), A.add)
        cp(B("offw", 0, 3), ys)
        nw = "w%d" % min(r + 1, RO - 1)
        cp(ind(v(nw, 0, DW + V), B("offw", 0, 3)), v("pw", 0, 16 * n3))
        if last:
            dma("s", T.y[:], T[nw][:, DW:DW + V], [(nw, DW, DW + V)], [("y", 0, 1)], 4.0)
            continue
        send_ghosts(r + 1)
        W = 16 * nc
        val, av, ev, z2, v2 = sm(n3), sm(2 * nc), sm(nc), sm(nc), sm(nc)
        fv = v("fv", 16 * r, 16 * r + nc)
        tt(val, B("bb", 0, 3), B("cc", 0, 3), A.add)
        tt(av, ask, v("sm", val[1][0][1], val[1][0][1] + 2 * nc), A.mult)
        tt(ev, part(av, 0), part(av, 1), A.add)
        tt(z2, B("reach", 2), B("stk", 2), A.mult)
        tt(v2, z2, part(val, 2), A.mult)
        tt(fv, v2, ev, A.add)
        tt(v("vx", 0, W), ind(fv, v("bc16", 0, nc)), v("diag", 0, W), A.mult)
        mm([(v("XX", 256, 256 + W), v("blkf"), v("vx", 0, W), True, True)])
        act(v("va", 0, W), v("XX", 256, 256 + W))
        anyd, d1, d2, t1, t3, t4 = sm(nc), sm(nc), sm(nc), sm(nc), sm(nc), sm(nc)
        ts(anyd, dd, 5.0, None, A.is_ge)
        ts(d1, dd, 32.0, DM - 160.0, A.mult, A.add)
        tt(d2, d1, v("pos", 0, nc), A.subtract)
        tt(t1, ro, d2, A.add)
        tt(t3, good, anyd, A.mult)
        tt(t4, t1, t3, A.mult)
        put(ind(v("ms%d" % r), offsets(t4, 0, nc)), v("va", 0, W))
        send_orders(r)
        fr = sm(nc)
        tt(fr, B("reach", 0), good, A.is_gt)
        requests(r + 1)
        for off in frozen:
            put(ind(v("mk%d" % (r + 1)), off), v("pzf", 0, 16 * off[2]))
        frozen.append(mark(r + 1, o0, 0, nc, fr, "pzf"))
    return ops


def arrange(ops):
    acc = {}
    n = len(ops)
    deps = [set() for _ in range(n)]
    for i, o in enumerate(ops):
        for regs, isw in ((o["r"], False), (o["w"], True)):
            for name, lo, hi in regs:
                if name in PSUM:
                    st = acc.setdefault(name, [o["e"], [], []])
                    if st[0] != o["e"]:
                        st[0], st[1], st[2] = o["e"], [], st[1]
                    deps[i].update(st[2])
                    st[1].append(i)
                    continue
                keep = []
                for e in acc.get(name, ()):
                    j, l2, h2, w2 = e
                    if j != i:
                        if l2 < hi and lo < h2 and (isw or w2):
                            deps[i].add(j)
                        if isw and lo <= l2 and h2 <= hi:
                            continue
                    keep.append(e)
                keep.append((i, lo, hi, isw))
                acc[name] = keep
    lastmm = {}
    for i, o in enumerate(ops):
        if o["e"] == "t":
            for name, lo, hi in o["w"]:
                if name in lastmm and lastmm[name] != i:
                    deps[i].add(lastmm[name])
                lastmm[name] = i
    loads = [i for i in range(n) if ops[i]["e"] == "s"]
    chain = set(zip(loads, loads[1:]))

    def lat(j, i):
        if ops[j]["e"] == ops[i]["e"] == "s" and j not in deps[i]:
            return 0.0
        if ops[j]["tok"]:
            return ops[j]["lat"]
        if ops[j]["e"] == ops[i]["e"]:
            return 0.0 if ops[j]["e"] == "t" else LSAME
        return LCROSS
    cost = [o["c"] for o in ops]
    before = [[(j, cost[j] + lat(j, i)) for j in deps[i]] for i in range(n)]
    for j, i in chain:
        if j not in deps[i]:
            before[i].append((j, cost[j]))
    after = [[] for _ in range(n)]
    for i in range(n):
        for j, d in before[i]:
            after[j].append((i, d - cost[j] + cost[i]))

    def place(seq, need, back):
        start = [0.0] * n
        slots = {e: [] for e in "vatgsx"}
        for i in seq:
            c = cost[i]
            t = ops[i]["lat"] if back else 0.0
            for j, d in need[i]:
                if start[j] + d > t:
                    t = start[j] + d
            sl = slots[ops[i]["e"]]
            k = len(sl)
            while k and sl[k - 1][1] > t:
                k -= 1
            while k < len(sl) and sl[k][0] < t + c:
                t = max(t, sl[k][1])
                k += 1
            sl.insert(k, (t, t + c))
            start[i] = t
        return start

    def sequence(key):
        low = list(key)
        for i in range(n):
            for j, d in before[i]:
                if low[j] >= low[i]:
                    low[i] = low[j] + 1e-6
        return sorted(range(n), key=lambda i: (low[i], i))
    if not ORDER:
        rng = np.random.RandomState(1)
        way = [0.0] * n
        for i in range(n - 1, -1, -1):
            way[i] = max([d - cost[u] + cost[i] + way[u] for u, d in after[i]] + [cost[i] + ops[i]["lat"]])
        key = [-x for x in way]
        best = None
        for it in range(TRIES):
            when = place(sequence(key), before, False)
            end = max(when[i] + cost[i] + ops[i]["lat"] for i in range(n))
            if best is None or end < best[0]:
                best = (end, when)
            elif it % 3 == 2:
                when = [x + y for x, y in zip(best[1], rng.uniform(0.0, 1.0, n).tolist())]
                when = place(sequence(when), before, False)
            late = place(sorted(range(n), key=lambda i: (-when[i] - cost[i], -i)), after, True)
            key = [-late[i] - cost[i] for i in range(n)]
        ORDER.append(best[1])
    when = ORDER[0]
    order = {e: sorted((i for i in range(n) if ops[i]["e"] == e), key=lambda i: (when[i], i)) for e in "vatgsx"}
    busy = {e: sum(cost[i] for i in order[e]) for e in order}
    return deps, order, when, busy


def rank_program(g, core, T, topo):
    rank = T.rank_of(core)
    if rank is None:
        return
    ops = build(T, rank, topo)
    deps, order, when, busy = arrange(ops)
    Q = {"v": g.vector, "a": g.scalar, "t": g.tensor, "g": g, "s": g.sync}
    tok = {}
    total = {}
    for e in "vatgsx":
        cnt = 0
        for i in order[e]:
            if ops[i]["tok"]:
                tok[i] = ops[i]["tok"]
            else:
                cnt += 1
                tok[i] = ("c" + e, cnt)
            total[tok[i][0]] = tok[i][1]
    known = {e: {} for e in Q}
    seen = {}
    for i in sorted(range(len(ops)), key=lambda j: (when[j], j)):
        o = ops[i]
        e = o["e"]
        if e == "x":
            seen[i] = {}
            continue
        kn = known[e]
        for j in sorted(deps[i], key=lambda j: -when[j]):
            if e == ops[j]["e"] == "t":
                continue
            s, val = tok[j]
            if kn.get(s, 0) < val:
                Q[e].wait_ge(T.sem[s], val)
                kn[s] = val
                for s2, v2 in seen[j].items():
                    if kn.get(s2, 0) < v2:
                        kn[s2] = v2
        seen[i] = dict(kn)
        ins = o["fn"](Q[e])
        if not (e == "g" and o["tok"]):
            ins.then_inc(T.sem[tok[i][0]], 16 if o["tok"] else 1)
    for s, val in total.items():
        g.sync.wait_ge(T.sem[s], val)
